import numpy as np
import ml_dtypes


def mxq(x, axis, fmt="e4m3"):
    dtype, down = {"e4m3": (ml_dtypes.float8_e4m3fn, 7), "e5m2": (ml_dtypes.float8_e5m2, 14)}[fmt]
    v = np.moveaxis(np.asarray(x, np.float32).astype(ml_dtypes.bfloat16).astype(np.float64), axis, -1)
    blocks = v.reshape(v.shape[:-1] + (-1, 32))
    amax = np.abs(blocks).max(-1, keepdims=True)
    byte = np.maximum(np.where(amax > 0, np.frexp(amax)[1] - 1 + 127, 0) - down, 1)
    scale = np.exp2(byte - 127.0)
    codes = (blocks / scale).astype(np.float32).astype(dtype).astype(np.float64)
    return np.moveaxis((codes * scale).reshape(v.shape), -1, axis)


WIDE = False


def mx_kscale(k):
    if not WIDE:
        return np.ones(k)
    levels = np.array([10, -10, 5, -5, 0])
    if k % 512:
        return np.exp2(np.random.permutation(np.resize(levels, k // 32))).repeat(32)
    a = np.empty((k // 512, 16))
    for p in range(k // 512):
        a[p, :8] = np.random.permutation(np.resize(levels, 8))
        for g in range(8):
            far = levels[np.abs(levels - a[p, g]) >= 10]
            a[p, g + 8] = far[np.random.randint(len(far))]
    return np.exp2(a.ravel()).repeat(32)


def f64(x):
    return np.asarray(x).astype(np.float64)


def striped(idx):
    return np.tile(idx.reshape(-1, 16).T, (8, 1)).astype(np.uint16)


def unstriped(offs):
    return offs[:16].T.reshape(-1).astype(np.int64)


def striped8(idx):
    return np.concatenate([x.reshape(-1, 16).T for x in idx]).astype(np.uint16)


def runs(offs, k):
    lists = np.stack([offs[16 * r : 16 * r + 16].T.reshape(-1) for r in range(8)]).astype(np.int64)
    return lists[np.arange(k) % 512 // 64]


def pack_weight(w):
    k, n = w.shape
    w = f64(np.asarray(w, np.float32).astype(ml_dtypes.bfloat16)).reshape(k // 32, 32, n)
    amax = np.abs(w).max(1)
    byte = np.clip(np.where(amax > 0, np.frexp(amax)[1] - 1 + 127 - 7, 1), 1, 254)
    scaled = (w * np.exp2(127.0 - byte)[:, None, :]).reshape(k, n).astype(np.float32)
    words = np.ascontiguousarray(scaled.reshape(k // 512, 128, 4, n).transpose(0, 1, 3, 2)).astype(ml_dtypes.float8_e4m3fn).view(np.uint8)
    return words, np.ascontiguousarray(byte.astype(np.uint8).reshape(k // 512, 16, n))


def unpack_weight(words, scales):
    g, p, n, _ = words.shape
    vals = np.ascontiguousarray(words).view(ml_dtypes.float8_e4m3fn).astype(np.float64) * np.repeat(np.exp2(scales.astype(np.float64) - 127.0), 8, axis=1)[..., None]
    return vals.transpose(0, 1, 3, 2).reshape(g * 512, n)


K, T, S, H, C, U = 512, 2048, 256, 512, 512, 512


def setup_inputs():
    n = np.random.standard_normal
    s = mx_kscale(K)[:, None]
    packed_xT = pack_weight(n((K, T)) * s)
    perm = np.random.permutation(U)
    return {
        "x_words": packed_xT[0],
        "x_scales": packed_xT[1],
        "w1": (n((K, H)) / np.sqrt(2 * K) / s).astype(np.float32),
        "w2": (n((K, H)) / np.sqrt(2 * K) / s).astype(np.float32),
        "gs": (np.random.uniform(0.5, 1.5, (K, 1)) / s).astype(np.float32),
        "offs": striped(np.random.permutation(T)[:S]),
        "hz": striped8(np.random.randint(0, T, (8, S))),
        "cand": striped(np.random.permutation(T)[:C]),
        "n1": striped(perm[:S]),
        "n2": striped(perm[S:]),
        "n3": striped(np.random.permutation(U)),
    }


def reference(x_words, x_scales, w1, w2, gs, offs, hz, cand, n1, n2, n3):
    x_cand = unpack_weight(x_words, x_scales)[:, unstriped(cand)]
    xq = unpack_weight(x_words, x_scales)[:, unstriped(offs)]
    x_hz = unpack_weight(x_words, x_scales)[np.arange(K)[:, None], runs(hz, K)]
    y = mxq(f64(w1), 0, "e4m3").T @ xq + mxq(f64(w2), 0, "e4m3").T @ x_hz
    z = f64(gs) * y
    s = 0.0625 * ((x_cand.T @ mxq(z, 0, "e4m3")))
    nw = 0.5 * s
    ph = np.zeros((C, U))
    ph[:, unstriped(n1)] = s
    pg = ph.copy()
    pg[:, unstriped(n2)] = nw
    return pg - pg[:, unstriped(n3)]

@@ -1,0 +1,203 @@
+from contextlib import ExitStack
+
+import concourse.mybir as mybir
+
+K, T, S, H, C, U = 512, 2048, 256, 512, 512, 512
+FLOPS = 2 * K * H * S * 2 + 2 * K * C * S
+
+F32 = mybir.dt.float32
+BF16 = mybir.dt.bfloat16
+I32 = mybir.dt.int32
+U32 = mybir.dt.uint32
+U16 = mybir.dt.uint16
+U8 = mybir.dt.uint8
+FP8X4 = mybir.dt.float8_e4m3fn_x4
+COPY = mybir.ActivationFunctionType.Copy
+MULT = mybir.AluOpType.mult
+SUBTRACT = mybir.AluOpType.subtract
+
+P = 128
+PACK = 4
+HALF = S // 2
+SCALAR_SHARE = (80, 48)
+
+
+def tile_picked_thcipagtwo_none_p_kernel(
+    tc, x_words, x_scales, w1, w2, gs, offs, hz, cand, n1, n2, n3, out
+):
+    nc = tc.nc
+    with ExitStack() as ctx:
+        keep = ctx.enter_context(tc.tile_pool(name="keep", bufs=1))
+        psum = ctx.enter_context(tc.psum_pool(name="psum", bufs=1))
+
+        def sb(name, cols, dtype):
+            return keep.tile([P, cols], dtype, name=name, align_bytes=64)
+
+        def load_list(name, src):
+            tile = keep.tile([P, src.shape[1]], U16, name=name)
+            nc.sync.dma_start(tile[:], src)
+            return tile
+
+        def entries(tile, start, count):
+            return tile[:, start // 16 : (start + count) // 16]
+
+        scale_table = sb("scale_table", T, U8)
+        nc.sync.dma_start(
+            scale_table[:].bitcast(I32),
+            x_scales[0].bitcast(I32).unsqueeze(1).to_broadcast([16, 8, T // 4]),
+        )
+
+        hz_list = load_list("hz_list", hz)
+        offs_list = load_list("offs_list", offs)
+        cand_list = load_list("cand_list", cand)
+
+        raw = []
+        for i, w in enumerate((w1, w2)):
+            tile = keep.tile([P, PACK, H], F32, name=f"w_raw{i}")
+            nc.sync.dma_start(tile[:], w.rearrange("(p j) c -> p j c", j=PACK))
+            raw.append(tile)
+        word_table = sb("word_table", T, U32)
+        nc.sync.dma_start(
+            word_table[:].bitcast(I32), x_words[0].rearrange("p n t -> p (n t)").bitcast(I32)
+        )
+        n1_list = load_list("n1_list", n1)
+        n2_list = load_list("n2_list", n2)
+        n3_list = load_list("n3_list", n3)
+        gain = keep.tile([P, PACK], F32, name="gain")
+        nc.gpsimd.dma_start(gain[:], gs.rearrange("(p t) o -> p (t o)", t=PACK))
+
+        def gather(name, table, offsets, count, dtype, tag=None):
+            tile = keep.tile([P, count], dtype, name=name, tag=tag or name, align_bytes=64)
+            nc.vector.tensor_copy(tile[:], table[:].indirect(offsets))
+            return tile
+
+        picked = sb("picked", 2 * S + C, U8)
+        start = 0
+        for offsets, count in ((offs_list, S), (hz_list, S), (cand_list, C)):
+            nc.vector.tensor_copy(picked[:, start : start + count], scale_table[:].indirect(offsets[:]))
+            start += count
+        placed = sb("placed", 2 * S + C, U8)
+        nc.vector.tensor_copy(placed[:].bitcast(I32), picked[:].bitcast(I32))
+        for r in range(1, 4):
+            nc.gpsimd.dma_start(placed[r:P:32, :].bitcast(I32), picked[8 * r : P : 32, :].bitcast(I32))
+        token_scales = placed[:, : 2 * S]
+        cand_scales = placed[:, 2 * S :]
+
+        w_codes, w_scales = [], []
+        for i in range(2):
+            grouped = sb(f"w_grouped{i}", PACK * H, BF16)
+            dst = grouped[:].rearrange("p (t m j) -> p m t j", t=PACK, j=PACK)
+            src = raw[i][:].rearrange("p j (m t) -> p m t j", t=PACK)
+            cut = SCALAR_SHARE[i]
+            nc.scalar.copy(dst[:, :cut], src[:, :cut])
+            nc.vector.tensor_copy(dst[:, cut:], src[:, cut:])
+            codes = sb(f"w_codes{i}", H, U32)
+            scales = sb(f"w_scales{i}", H, U8)
+            nc.vector.quantize_mx(codes[:].bitcast(FP8X4), scales[:], grouped[:])
+            w_codes.append(codes)
+            w_scales.append(scales)
+
+        def first_product(h, offs_words):
+            cols = slice(h * HALF, (h + 1) * HALF)
+            y = psum.tile([P, PACK, HALF], F32, name=f"y{h}")
+            moving = (
+                (offs_words[:], token_scales[:, h * HALF : (h + 1) * HALF]),
+                (hz_words[:, cols], token_scales[:, S + h * HALF : S + (h + 1) * HALF]),
+            )
+            passes = [(0, 0), (0, 1), (0, 2), (1, 0), (1, 1), (1, 2), (1, 3), (0, 3)]
+            for n, (i, t) in enumerate(passes):
+                nc.tensor.matmul_mx(
+                    y[:, t, :],
+                    lhsT=w_codes[i][:, t * P : (t + 1) * P].bitcast(FP8X4),
+                    lhsT_scale=w_scales[i][:, t * P : (t + 1) * P],
+                    rhs=moving[i][0].bitcast(FP8X4),
+                    rhs_scale=moving[i][1],
+                    start=(n == 0),
+                    stop=(n == len(passes) - 1),
+                )
+            return y
+
+        z_codes = sb("z_codes", S, U32)
+        z_scales = sb("z_scales", S, U8)
+
+        def weigh(h, y):
+            z = keep.tile([P, HALF, PACK], BF16, name=f"z{h}", align_bytes=64)
+            nc.vector.tensor_tensor(
+                z[:],
+                y[:].rearrange("p t n -> p n t"),
+                gain[:].unsqueeze(1).to_broadcast([P, HALF, PACK]),
+                MULT,
+            )
+            return z
+
+        def quantize_z(h, z):
+            cols = slice(h * HALF, (h + 1) * HALF)
+            nc.vector.quantize_mx(
+                z_codes[:, cols].bitcast(FP8X4), z_scales[:, cols], z[:].rearrange("p n t -> p (n t)")
+            )
+
+        def scores(name, pair, start, count):
+            cols = slice(start, start + count)
+            acc = psum.tile([P, 2, count], F32, name=f"acc_{name}")
+            for b in range(2):
+                nc.tensor.matmul_mx(
+                    acc[:, b, :],
+                    lhsT=cand_words[pair][:, b * P : (b + 1) * P].bitcast(FP8X4),
+                    lhsT_scale=cand_scales[:, (2 * pair + b) * P : (2 * pair + b + 1) * P],
+                    rhs=z_codes[:, cols].bitcast(FP8X4),
+                    rhs_scale=z_scales[:, cols],
+                    start=True,
+                    stop=True,
+                )
+            s = keep.tile([P, 2, count], F32, name=f"s_{name}")
+            nc.vector.tensor_scalar_mul(s[:], acc[:], 0.0625)
+            return s
+
+        pages = [sb(f"page{b}", U, F32) for b in range(C // P)]
+
+        def scatter(pair, s, start, count):
+            for slots, factor in ((n1_list, 1.0), (n2_list, 0.5)):
+                for b in range(2):
+                    nc.scalar.activation(
+                        pages[2 * pair + b][:].indirect(entries(slots, start, count)),
+                        s[:, b, :],
+                        COPY,
+                        scale=factor,
+                    )
+
+        def finish(b, widths):
+            start = 0
+            for width in widths:
+                cols = slice(start, start + width)
+                other = sb(f"other{b}_{start}", width, F32)
+                for g in range(0, width, S):
+                    n = min(S, width - g)
+                    nc.scalar.activation(
+                        other[:, g : g + n], pages[b][:].indirect(entries(n3_list, start + g, n)), COPY
+                    )
+                result = sb(f"result{b}_{start}", width, F32)
+                nc.vector.tensor_tensor(result[:], pages[b][:, cols], other[:], SUBTRACT)
+                nc.sync.dma_start(out[b * P : (b + 1) * P, cols], result[:])
+                start += width
+
+        offs_words0 = gather("offs_words0", word_table, entries(offs_list, 0, HALF), HALF, U32, "offs_words")
+        hz_words = gather("hz_words", word_table, hz_list[:], S, U32)
+        y0 = first_product(0, offs_words0)
+        cand_words = [gather("cand_words0", word_table, entries(cand_list, 0, 2 * P), 2 * P, U32)]
+        z0 = weigh(0, y0)
+        offs_words1 = gather("offs_words1", word_table, entries(offs_list, HALF, HALF), HALF, U32, "offs_words")
+        quantize_z(0, z0)
+        s_a = scores("a", 0, 0, HALF)
+        y1 = first_product(1, offs_words1)
+        scatter(0, s_a, 0, HALF)
+        z1 = weigh(1, y1)
+        quantize_z(1, z1)
+        cand_words.append(gather("cand_words1", word_table, entries(cand_list, 2 * P, 2 * P), 2 * P, U32, "hz_words"))
+        s_b = scores("b", 0, HALF, HALF)
+        scatter(0, s_b, HALF, HALF)
+        s_c = scores("c", 1, 0, S)
+        finish(0, (U,))
+        finish(1, (U,))
+        scatter(1, s_c, 0, S)
+        finish(2, (U,))
+        finish(3, (S, HALF, HALF))

@@ -79,7 +79,7 @@ def tile_picked_thcipagtwo_none_p_kernel(
         placed = sb("placed", 2 * S + C, U8)
         nc.vector.tensor_copy(placed[:].bitcast(I32), picked[:].bitcast(I32))
         for r in range(1, 4):
-            nc.gpsimd.dma_start(placed[r:P:32, :].bitcast(I32), picked[8 * r : P : 32, :].bitcast(I32))
+            nc.sync.dma_start(placed[r:P:32, :].bitcast(I32), picked[8 * r : P : 32, :].bitcast(I32))
         token_scales = placed[:, : 2 * S]
         cand_scales = placed[:, 2 * S :]
 

@@ -19,6 +19,7 @@ SUBTRACT = mybir.AluOpType.subtract
 P = 128
 PACK = 4
 HALF = S // 2
+QUARTER = S // 4
 SCALAR_SHARE = (80, 48)
 
 
@@ -89,7 +90,8 @@ def tile_picked_thcipagtwo_none_p_kernel(
             dst = grouped[:].rearrange("p (t m j) -> p m t j", t=PACK, j=PACK)
             src = raw[i][:].rearrange("p j (m t) -> p m t j", t=PACK)
             cut = SCALAR_SHARE[i]
-            nc.scalar.copy(dst[:, :cut], src[:, :cut])
+            if cut:
+                nc.scalar.copy(dst[:, :cut], src[:, :cut])
             nc.vector.tensor_copy(dst[:, cut:], src[:, cut:])
             codes = sb(f"w_codes{i}", H, U32)
             scales = sb(f"w_scales{i}", H, U8)
@@ -120,18 +122,18 @@ def tile_picked_thcipagtwo_none_p_kernel(
         z_codes = sb("z_codes", S, U32)
         z_scales = sb("z_scales", S, U8)
 
-        def weigh(h, y):
-            z = keep.tile([P, HALF, PACK], BF16, name=f"z{h}", align_bytes=64)
+        def weigh(y, start, count):
+            z = keep.tile([P, count, PACK], BF16, name=f"z{start}", align_bytes=64)
             nc.vector.tensor_tensor(
                 z[:],
-                y[:].rearrange("p t n -> p n t"),
-                gain[:].unsqueeze(1).to_broadcast([P, HALF, PACK]),
+                y[:, :, start % HALF : start % HALF + count].rearrange("p t n -> p n t"),
+                gain[:].unsqueeze(1).to_broadcast([P, count, PACK]),
                 MULT,
             )
             return z
 
-        def quantize_z(h, z):
-            cols = slice(h * HALF, (h + 1) * HALF)
+        def quantize_z(z, start, count):
+            cols = slice(start, start + count)
             nc.vector.quantize_mx(
                 z_codes[:, cols].bitcast(FP8X4), z_scales[:, cols], z[:].rearrange("p n t -> p (n t)")
             )
@@ -184,20 +186,19 @@ def tile_picked_thcipagtwo_none_p_kernel(
         hz_words = gather("hz_words", word_table, hz_list[:], S, U32)
         y0 = first_product(0, offs_words0)
         cand_words = [gather("cand_words0", word_table, entries(cand_list, 0, 2 * P), 2 * P, U32)]
-        z0 = weigh(0, y0)
+        z = weigh(y0, 0, QUARTER)
         offs_words1 = gather("offs_words1", word_table, entries(offs_list, HALF, HALF), HALF, U32, "offs_words")
-        quantize_z(0, z0)
-        s_a = scores("a", 0, 0, HALF)
+        quantize_z(z, 0, QUARTER)
+        scatter(0, scores("a", 0, 0, QUARTER), 0, QUARTER)
+        quantize_z(weigh(y0, QUARTER, QUARTER), QUARTER, QUARTER)
+        scatter(0, scores("b", 0, QUARTER, QUARTER), QUARTER, QUARTER)
         y1 = first_product(1, offs_words1)
-        scatter(0, s_a, 0, HALF)
-        z1 = weigh(1, y1)
-        quantize_z(1, z1)
+        quantize_z(weigh(y1, HALF, HALF), HALF, HALF)
         cand_words.append(gather("cand_words1", word_table, entries(cand_list, 2 * P, 2 * P), 2 * P, U32, "hz_words"))
-        s_b = scores("b", 0, HALF, HALF)
-        scatter(0, s_b, HALF, HALF)
+        scatter(0, scores("d", 0, HALF, HALF), HALF, HALF)
         s_c = scores("c", 1, 0, S)
         finish(0, (U,))
         finish(1, (U,))
         scatter(1, s_c, 0, S)
         finish(2, (U,))
-        finish(3, (S, HALF, HALF))
+        finish(3, (S, S - QUARTER, QUARTER))

from contextlib import ExitStack

import concourse.mybir as mybir

K, T, S, H, C, U = 512, 2048, 256, 512, 512, 512
FLOPS = 2 * K * H * S * 2 + 2 * K * C * S

F32 = mybir.dt.float32
BF16 = mybir.dt.bfloat16
I32 = mybir.dt.int32
U32 = mybir.dt.uint32
U16 = mybir.dt.uint16
U8 = mybir.dt.uint8
FP8X4 = mybir.dt.float8_e4m3fn_x4
COPY = mybir.ActivationFunctionType.Copy
MULT = mybir.AluOpType.mult
SUBTRACT = mybir.AluOpType.subtract

P = 128
PACK = 4
HALF = S // 2
QUARTER = S // 4
SCALAR_SHARE = (80, 48)


def tile_picked_thcipagtwo_none_p_kernel(
    tc, x_words, x_scales, w1, w2, gs, offs, hz, cand, n1, n2, n3, out
):
    nc = tc.nc
    with ExitStack() as ctx:
        keep = ctx.enter_context(tc.tile_pool(name="keep", bufs=1))
        psum = ctx.enter_context(tc.psum_pool(name="psum", bufs=1))

        def sb(name, cols, dtype):
            return keep.tile([P, cols], dtype, name=name, align_bytes=64)

        def load_list(name, src):
            tile = keep.tile([P, src.shape[1]], U16, name=name)
            nc.sync.dma_start(tile[:], src)
            return tile

        def entries(tile, start, count):
            return tile[:, start // 16 : (start + count) // 16]

        scale_table = sb("scale_table", T, U8)
        nc.sync.dma_start(
            scale_table[:].bitcast(I32),
            x_scales[0].bitcast(I32).unsqueeze(1).to_broadcast([16, 8, T // 4]),
        )

        hz_list = load_list("hz_list", hz)
        offs_list = load_list("offs_list", offs)
        cand_list = load_list("cand_list", cand)

        raw = []
        for i, w in enumerate((w1, w2)):
            tile = keep.tile([P, PACK, H], F32, name=f"w_raw{i}")
            nc.sync.dma_start(tile[:], w.rearrange("(p j) c -> p j c", j=PACK))
            raw.append(tile)
        word_table = sb("word_table", T, U32)
        nc.sync.dma_start(
            word_table[:].bitcast(I32), x_words[0].rearrange("p n t -> p (n t)").bitcast(I32)
        )
        n1_list = load_list("n1_list", n1)
        n2_list = load_list("n2_list", n2)
        n3_list = load_list("n3_list", n3)
        gain = keep.tile([P, PACK], F32, name="gain")
        nc.gpsimd.dma_start(gain[:], gs.rearrange("(p t) o -> p (t o)", t=PACK))

        def gather(name, table, offsets, count, dtype, tag=None):
            tile = keep.tile([P, count], dtype, name=name, tag=tag or name, align_bytes=64)
            nc.vector.tensor_copy(tile[:], table[:].indirect(offsets))
            return tile

        picked = sb("picked", 2 * S + C, U8)
        start = 0
        for offsets, count in ((offs_list, S), (hz_list, S), (cand_list, C)):
            nc.vector.tensor_copy(picked[:, start : start + count], scale_table[:].indirect(offsets[:]))
            start += count
        placed = sb("placed", 2 * S + C, U8)
        nc.vector.tensor_copy(placed[:].bitcast(I32), picked[:].bitcast(I32))
        for r in range(1, 4):
            nc.sync.dma_start(placed[r:P:32, :].bitcast(I32), picked[8 * r : P : 32, :].bitcast(I32))
        token_scales = placed[:, : 2 * S]
        cand_scales = placed[:, 2 * S :]

        w_codes, w_scales = [], []
        for i in range(2):
            grouped = sb(f"w_grouped{i}", PACK * H, BF16)
            dst = grouped[:].rearrange("p (t m j) -> p m t j", t=PACK, j=PACK)
            src = raw[i][:].rearrange("p j (m t) -> p m t j", t=PACK)
            cut = SCALAR_SHARE[i]
            if cut:
                nc.scalar.copy(dst[:, :cut], src[:, :cut])
            nc.vector.tensor_copy(dst[:, cut:], src[:, cut:])
            codes = sb(f"w_codes{i}", H, U32)
            scales = sb(f"w_scales{i}", H, U8)
            nc.vector.quantize_mx(codes[:].bitcast(FP8X4), scales[:], grouped[:])
            w_codes.append(codes)
            w_scales.append(scales)

        def first_product(h, offs_words):
            cols = slice(h * HALF, (h + 1) * HALF)
            y = psum.tile([P, PACK, HALF], F32, name=f"y{h}")
            moving = (
                (offs_words[:], token_scales[:, h * HALF : (h + 1) * HALF]),
                (hz_words[:, cols], token_scales[:, S + h * HALF : S + (h + 1) * HALF]),
            )
            passes = [(0, 0), (0, 1), (0, 2), (1, 0), (1, 1), (1, 2), (1, 3), (0, 3)]
            for n, (i, t) in enumerate(passes):
                nc.tensor.matmul_mx(
                    y[:, t, :],
                    lhsT=w_codes[i][:, t * P : (t + 1) * P].bitcast(FP8X4),
                    lhsT_scale=w_scales[i][:, t * P : (t + 1) * P],
                    rhs=moving[i][0].bitcast(FP8X4),
                    rhs_scale=moving[i][1],
                    start=(n == 0),
                    stop=(n == len(passes) - 1),
                )
            return y

        z_codes = sb("z_codes", S, U32)
        z_scales = sb("z_scales", S, U8)

        def weigh(y, start, count):
            z = keep.tile([P, count, PACK], BF16, name=f"z{start}", align_bytes=64)
            nc.vector.tensor_tensor(
                z[:],
                y[:, :, start % HALF : start % HALF + count].rearrange("p t n -> p n t"),
                gain[:].unsqueeze(1).to_broadcast([P, count, PACK]),
                MULT,
            )
            return z

        def quantize_z(z, start, count):
            cols = slice(start, start + count)
            nc.vector.quantize_mx(
                z_codes[:, cols].bitcast(FP8X4), z_scales[:, cols], z[:].rearrange("p n t -> p (n t)")
            )

        def scores(name, pair, start, count):
            cols = slice(start, start + count)
            acc = psum.tile([P, 2, count], F32, name=f"acc_{name}")
            for b in range(2):
                nc.tensor.matmul_mx(
                    acc[:, b, :],
                    lhsT=cand_words[pair][:, b * P : (b + 1) * P].bitcast(FP8X4),
                    lhsT_scale=cand_scales[:, (2 * pair + b) * P : (2 * pair + b + 1) * P],
                    rhs=z_codes[:, cols].bitcast(FP8X4),
                    rhs_scale=z_scales[:, cols],
                    start=True,
                    stop=True,
                )
            s = keep.tile([P, 2, count], F32, name=f"s_{name}")
            nc.vector.tensor_scalar_mul(s[:], acc[:], 0.0625)
            return s

        pages = [sb(f"page{b}", U, F32) for b in range(C // P)]

        def scatter(pair, s, start, count):
            for slots, factor in ((n1_list, 1.0), (n2_list, 0.5)):
                for b in range(2):
                    nc.scalar.activation(
                        pages[2 * pair + b][:].indirect(entries(slots, start, count)),
                        s[:, b, :],
                        COPY,
                        scale=factor,
                    )

        def finish(b, widths):
            start = 0
            for width in widths:
                cols = slice(start, start + width)
                other = sb(f"other{b}_{start}", width, F32)
                for g in range(0, width, S):
                    n = min(S, width - g)
                    nc.scalar.activation(
                        other[:, g : g + n], pages[b][:].indirect(entries(n3_list, start + g, n)), COPY
                    )
                result = sb(f"result{b}_{start}", width, F32)
                nc.vector.tensor_tensor(result[:], pages[b][:, cols], other[:], SUBTRACT)
                nc.sync.dma_start(out[b * P : (b + 1) * P, cols], result[:])
                start += width

        offs_words0 = gather("offs_words0", word_table, entries(offs_list, 0, HALF), HALF, U32, "offs_words")
        hz_words = gather("hz_words", word_table, hz_list[:], S, U32)
        y0 = first_product(0, offs_words0)
        cand_words = [gather("cand_words0", word_table, entries(cand_list, 0, 2 * P), 2 * P, U32)]
        z = weigh(y0, 0, QUARTER)
        offs_words1 = gather("offs_words1", word_table, entries(offs_list, HALF, HALF), HALF, U32, "offs_words")
        quantize_z(z, 0, QUARTER)
        scatter(0, scores("a", 0, 0, QUARTER), 0, QUARTER)
        quantize_z(weigh(y0, QUARTER, QUARTER), QUARTER, QUARTER)
        scatter(0, scores("b", 0, QUARTER, QUARTER), QUARTER, QUARTER)
        y1 = first_product(1, offs_words1)
        quantize_z(weigh(y1, HALF, HALF), HALF, HALF)
        cand_words.append(gather("cand_words1", word_table, entries(cand_list, 2 * P, 2 * P), 2 * P, U32, "hz_words"))
        scatter(0, scores("d", 0, HALF, HALF), HALF, HALF)
        s_c = scores("c", 1, 0, S)
        finish(0, (U,))
        finish(1, (U,))
        scatter(1, s_c, 0, S)
        finish(2, (U,))
        finish(3, (S, S - QUARTER, QUARTER))
